import numpy as np
CORES = [0,1,2,3,4,5,6,7,8,9,10,11,12,13,14,15,16,17,18,19,20,21,22,23,24,25,26,27,28,29,30,31,32,33,34,35,36,37,38,39,40,41,42,43,44,45,46,47,48,49,50,51,52,53,54,55,56,57,58,59,60,61,62,63,64,65,66,67,68,69,70,71,72,73,74,75,76,77,78,79,80,81,82,83,84,85,86,87,88,89,90,91,92,93,94,95,96,97,98,99,100,101,102,103,104,105,106,107,108,109,110,111,112,113,114,115,116,117,118,119,120,121,122,123,124,125,126,127,128,129,130,131,132,133,134,135,136,137,138,139,140,141,142,143,144,145,146,147,148,149,150,151,152,153,154,155,156,157,158,159,160,161,162,163,164,165,166,167,168,169,170,171,172,173,174,175,176,177,178,179,180,181,182,183,184,185,186,187,188,189,190,191,192,193,194,195,196,197,198,199,200,201,202,203,204,205,206,207,208,209,210,211,212,213,214,215,216,217,218,219,220,221,222,223,224,225,226,227,228,229,230,231,232,233,234,235,236,237,238,239,240,241,242,243,244,245,246,247,248,249,250,251,252,253,254,255,256,257,258,259,260,261,262,263,264,265,266,267,268,269,270,271,272,273,274,275,276,277,278,279,280,281,282,283,284,285,286,287,288,289,290,291,292,293,294,295,296,297,298,299,300,301,302,303,304,305,306,307,308,309,310,311,312,313,314,315,316,317,318,319,320,321,322,323,324,325,326,327,328,329,330,331,332,333,334,335,336,337,338,339,340,341,342,343,344,345,346,347,348,349,350,351,352,353,354,355,356,357,358,359,360,361,362,363,364,365,366,367,368,369,370,371,372,373,374,375,376,377,378,379,380,381,382,383,384,385,386,387,388,389,390,391,392,393,394,395,396,397,398,399,400,401,402,403,404,405,406,407,408,409,410,411,412,413,414,415,416,417,418,419,420,421,422,423,424,425,426,427,428,429,430,431,432,433,434,435,436,437,438,439,440,441,442,443,444,445,446,447,448,449,450,451,452,453,454,455,456,457,458,459,460,461,462,463,464,465,466,467,468,469,470,471,472,473,474,475,476,477,478,479,480,481,482,483,484,485,486,487,488,489,490,491,492,493,494,495,496,497,498,499,500,501,502,503,504,505,506,507,508,509,510,511]
N = 512
STEPS = 2
def setup_inputs(rng):
    return {"x": rng.standard_normal((N, 128, 512)).astype(np.float32)}
def reference(x):
    line = np.concatenate(list(x.astype(np.float64)), axis=1)
    for _ in range(STEPS):
        line = np.roll(line, 1, axis=1) + line + np.roll(line, -1, axis=1)
    return {"y": np.stack(np.split(line, N, axis=1)).astype(x.dtype)}

from concourse.bass import DstId, RemoteDMATransfer
from concourse.mybir import AluOpType

W = 512
H = 2

SCRATCH = {
    "ext": ("sbuf", [128, W + 2 * H], "float32"),
    "mid": ("sbuf", [128, W + 2], "float32"),
    "fwd": ("sbuf", [128, H], "float32"),
}
SEMAPHORES = ["step", "sent", "halo", "relay"]

RELAY = 2


def rank_program(g, core, T, topo):
    rank = T.rank_of(core)
    if rank is None:
        return
    n = len(T.cores)

    def left_of(c):
        return T.cores[(T.rank_of(c) - 1) % n]

    def right_of(c):
        return T.cores[(T.rank_of(c) + 1) % n]

    left, right = left_of(core), right_of(core)
    head = core - core % 8
    sem = T.sem
    ext, mid = T.ext, T.mid

    done = [0]

    def local(out, in_, add=False):
        if add:
            g.dma_start(out, in_, accum_op=AluOpType.add).then_inc(sem.step, 16)
        else:
            g.dma_start(out, in_).then_inc(sem.step, 16)
        done[0] += 16
        g.wait_ge(sem.step, done[0])

    transfers = []

    def send(dst_core, dst_ap, src_ap, remote_sem):
        rid, pid = topo.addr(dst_core, core)
        transfers.append(RemoteDMATransfer(
            dst_ids=[DstId(rid=rid, pnc=pid)], dma_engine_mask=1 << len(transfers),
            remote_sem=remote_sem, src=src_ap, dst=dst_ap, alu_op=0))

    local(ext[:, H:H + W], T.x[:, :])

    if core % 8 == RELAY and not topo.may_write(head, left_of(head)):
        g.wait_ge(sem.relay, 1)
        send(left_of(head), ext[:, H + W:H + W + H], T.fwd[:, :], sem.halo)

    send(right, ext[:, 0:H], ext[:, W:W + H], sem.halo)

    if topo.may_write(core, left):
        send(left, ext[:, H + W:H + W + H], ext[:, H:2 * H], sem.halo)
    else:
        send(head + RELAY, T.fwd[:, :], ext[:, H:2 * H], sem.relay)

    g.remote_dma_fused(transfers, local_sem=sem.sent)

    g.wait_ge(sem.halo, 2)

    local(mid[:, :], ext[:, 0:W + 2])
    local(mid[:, :], ext[:, 1:W + 3], add=True)
    local(mid[:, :], ext[:, 2:W + 4], add=True)
    local(T.y[:, :], mid[:, 0:W])
    local(T.y[:, :], mid[:, 1:W + 1], add=True)
    local(T.y[:, :], mid[:, 2:W + 2], add=True)

    g.wait_ge(sem.sent, len(transfers))
